import numpy as np
import ml_dtypes

BF16 = ml_dtypes.bfloat16


def bf(x):
    return np.asarray(x, np.float32).astype(BF16)


def f32(x):
    return np.asarray(x, np.float32)


def f64(x):
    return np.asarray(x).astype(np.float64)


def striped(idx):
    return np.tile(idx.reshape(-1, 16).T, (8, 1))


def rows(idx, k):
    return np.tile(idx, (k, 1))


def look(tab, idx):
    return np.take_along_axis(f64(tab), rows(idx, len(tab)), axis=1)


K, S, V, N, M = 256, 2048, 1536, 1536, 256


def setup_inputs():
    return {"tab": f32(np.random.standard_normal((2, K, S))), "y": f32(1.0 * np.random.standard_normal((K, V))), "w": bf(np.random.standard_normal((K, M)) / np.sqrt(K)), "b": f32(0.5 * np.random.standard_normal((M, 1))), "offs": striped(np.random.permutation(S)[:N])}


def reference(tab, y, w, b, offs):
    idx = offs[:16].T.reshape(-1)
    x = np.maximum(look(tab[0], idx), f64(y)) * np.tanh(look(tab[1], idx))
    return np.maximum(f64(w).T @ x + f64(b), 0.0)

@@ -1,0 +1,71 @@
+import concourse.mybir as mybir
+
+P = 128
+PIECE = 512
+FLOPS = 2 * 256 * 256 * 1536
+F32, BF16, U16 = mybir.dt.float32, mybir.dt.bfloat16, mybir.dt.uint16
+
+
+def tile_lookup_maxgate_relu_kernel(tc, tab, y, w, b, offs, out):
+    nc = tc.nc
+    maximum, mult = mybir.AluOpType.max, mybir.AluOpType.mult
+    tanh, relu = mybir.ActivationFunctionType.Tanh, mybir.ActivationFunctionType.Relu
+
+    rows, places = tab.shape[1], tab.shape[2]
+    picks = y.shape[1]
+    outs = w.shape[1]
+    row_blocks, out_blocks, pieces = rows // P, outs // P, picks // PIECE
+
+    with (
+        tc.tile_pool(name="held", bufs=1) as held,
+        tc.tile_pool(name="work", bufs=pieces) as work,
+        tc.psum_pool(name="psum", bufs=1) as psum,
+    ):
+        offsets = held.tile([P, picks // 16], U16)
+        nc.sync.dma_start(offsets[:], offs)
+
+        floors, gates, stream = [], [], []
+        for k in range(row_blocks):
+            block = slice(k * P, (k + 1) * P)
+            floors.append(held.tile([P, places], F32, name=f"floors{k}"))
+            stream.append(held.tile([P, picks], F32, name=f"stream{k}"))
+            gates.append(held.tile([P, places], F32, name=f"gates{k}"))
+            nc.sync.dma_start(floors[k][:], tab[0, block, :])
+            nc.sync.dma_start(stream[k][:], y[block, :])
+            nc.sync.dma_start(gates[k][:], tab[1, block, :])
+
+        weights = [held.tile([P, outs], BF16, name=f"weights{k}") for k in range(row_blocks)]
+        for k in range(row_blocks):
+            nc.scalar.dma_start(weights[k][:], w[k * P : (k + 1) * P, :])
+        bias = held.tile([P, out_blocks], F32)
+        nc.scalar.dma_start(bias[:], b.rearrange("(m p) one -> p (m one)", p=P))
+
+        sums = [[psum.tile([P, PIECE], F32, name=f"sum{m}_{c}") for c in range(pieces)] for m in range(out_blocks)]
+
+        for k in range(row_blocks):
+            for c in range(pieces):
+                cols = slice(c * PIECE, (c + 1) * PIECE)
+                picked = offsets[:, c * PIECE // 16 : (c + 1) * PIECE // 16]
+
+                floored = work.tile([P, PIECE], F32)
+                nc.vector.tensor_tensor(floored[:], floors[k][:].indirect(picked), stream[k][:, cols], maximum)
+                gate = work.tile([P, PIECE], F32)
+                nc.scalar.activation(gate[:], gates[k][:].indirect(picked), tanh)
+                x = work.tile([P, PIECE], BF16)
+                nc.vector.tensor_tensor(x[:], floored[:], gate[:], mult)
+
+                for m in range(out_blocks):
+                    nc.tensor.matmul(
+                        sums[m][c][:],
+                        weights[k][:, m * P : (m + 1) * P],
+                        x[:],
+                        start=(k == 0),
+                        stop=(k == row_blocks - 1),
+                    )
+
+        for c in range(pieces):
+            cols = slice(c * PIECE, (c + 1) * PIECE)
+            for m in range(out_blocks):
+                result = work.tile([P, PIECE], F32, name=f"result{m}")
+                nc.scalar.activation(result[:], sums[m][c][:], relu, bias=bias[:, m : m + 1])
+                nc.sync.dma_start(out[m * P : (m + 1) * P, cols], result[:])

@@ -21,34 +21,40 @@ def tile_lookup_maxgate_relu_kernel(tc, tab, y, w, b, offs, out):
         tc.tile_pool(name="work", bufs=pieces) as work,
         tc.psum_pool(name="psum", bufs=1) as psum,
     ):
+        zeros = held.tile([P, 1], F32)
+        nc.vector.memset(zeros[:], 0.0)
+        warm_up = held.tile([P, 1], F32)
+        nc.scalar.activation(warm_up[:], zeros[:], tanh)
+
         offsets = held.tile([P, picks // 16], U16)
         nc.sync.dma_start(offsets[:], offs)
 
+        weights = [held.tile([P, outs], BF16, name=f"weights{k}") for k in range(row_blocks)]
+        bias = held.tile([P, out_blocks], F32)
         floors, gates, stream = [], [], []
         for k in range(row_blocks):
             block = slice(k * P, (k + 1) * P)
             floors.append(held.tile([P, places], F32, name=f"floors{k}"))
-            stream.append(held.tile([P, picks], F32, name=f"stream{k}"))
             gates.append(held.tile([P, places], F32, name=f"gates{k}"))
+            stream.append([held.tile([P, PIECE], F32, name=f"stream{k}_{c}") for c in range(pieces)])
             nc.sync.dma_start(floors[k][:], tab[0, block, :])
-            nc.sync.dma_start(stream[k][:], y[block, :])
-            nc.sync.dma_start(gates[k][:], tab[1, block, :])
-
-        weights = [held.tile([P, outs], BF16, name=f"weights{k}") for k in range(row_blocks)]
-        for k in range(row_blocks):
-            nc.scalar.dma_start(weights[k][:], w[k * P : (k + 1) * P, :])
-        bias = held.tile([P, out_blocks], F32)
+            for c in range(pieces):
+                if c == pieces - 1:
+                    nc.sync.dma_start(gates[k][:], tab[1, block, :])
+                nc.sync.dma_start(stream[k][c][:], y[block, c * PIECE : (c + 1) * PIECE])
+            if k == 0:
+                for i in range(row_blocks):
+                    nc.sync.dma_start(weights[i][:], w[i * P : (i + 1) * P, :])
         nc.scalar.dma_start(bias[:], b.rearrange("(m p) one -> p (m one)", p=P))
 
         sums = [[psum.tile([P, PIECE], F32, name=f"sum{m}_{c}") for c in range(pieces)] for m in range(out_blocks)]
 
         for k in range(row_blocks):
             for c in range(pieces):
-                cols = slice(c * PIECE, (c + 1) * PIECE)
                 picked = offsets[:, c * PIECE // 16 : (c + 1) * PIECE // 16]
 
                 floored = work.tile([P, PIECE], F32)
-                nc.vector.tensor_tensor(floored[:], floors[k][:].indirect(picked), stream[k][:, cols], maximum)
+                nc.vector.tensor_tensor(floored[:], floors[k][:].indirect(picked), stream[k][c][:], maximum)
                 gate = work.tile([P, PIECE], F32)
                 nc.scalar.activation(gate[:], gates[k][:].indirect(picked), tanh)
                 x = work.tile([P, PIECE], BF16)
@@ -62,10 +68,16 @@ def tile_lookup_maxgate_relu_kernel(tc, tab, y, w, b, offs, out):
                         start=(k == 0),
                         stop=(k == row_blocks - 1),
                     )
+                if k < row_blocks - 1:
+                    continue
 
-        for c in range(pieces):
-            cols = slice(c * PIECE, (c + 1) * PIECE)
-            for m in range(out_blocks):
-                result = work.tile([P, PIECE], F32, name=f"result{m}")
-                nc.scalar.activation(result[:], sums[m][c][:], relu, bias=bias[:, m : m + 1])
-                nc.sync.dma_start(out[m * P : (m + 1) * P, cols], result[:])
+                cols = slice(c * PIECE, (c + 1) * PIECE)
+                for m in range(out_blocks):
+                    result = work.tile([P, PIECE], F32, name=f"result{m}")
+                    if m % 2 == 0:
+                        nc.vector.tensor_scalar(
+                            result[:], sums[m][c][:], bias[:, m : m + 1], 0.0, mybir.AluOpType.add, maximum
+                        )
+                    else:
+                        nc.scalar.activation(result[:], sums[m][c][:], relu, bias=bias[:, m : m + 1])
+                    nc.sync.dma_start(out[m * P : (m + 1) * P, cols], result[:])

@@ -37,10 +37,12 @@ def tile_lookup_maxgate_relu_kernel(tc, tab, y, w, b, offs, out):
             floors.append(held.tile([P, places], F32, name=f"floors{k}"))
             gates.append(held.tile([P, places], F32, name=f"gates{k}"))
             stream.append([held.tile([P, PIECE], F32, name=f"stream{k}_{c}") for c in range(pieces)])
+            pieces_ahead = pieces if k < row_blocks - 1 else 1
             nc.sync.dma_start(floors[k][:], tab[0, block, :])
-            for c in range(pieces):
-                if c == pieces - 1:
-                    nc.sync.dma_start(gates[k][:], tab[1, block, :])
+            for c in range(pieces_ahead):
+                nc.sync.dma_start(stream[k][c][:], y[block, c * PIECE : (c + 1) * PIECE])
+            nc.sync.dma_start(gates[k][:], tab[1, block, :])
+            for c in range(pieces_ahead, pieces):
                 nc.sync.dma_start(stream[k][c][:], y[block, c * PIECE : (c + 1) * PIECE])
             if k == 0:
                 for i in range(row_blocks):
@@ -74,7 +76,7 @@ def tile_lookup_maxgate_relu_kernel(tc, tab, y, w, b, offs, out):
                 cols = slice(c * PIECE, (c + 1) * PIECE)
                 for m in range(out_blocks):
                     result = work.tile([P, PIECE], F32, name=f"result{m}")
-                    if m % 2 == 0:
+                    if c == pieces - 1 and m % 2 == 0:
                         nc.vector.tensor_scalar(
                             result[:], sums[m][c][:], bias[:, m : m + 1], 0.0, mybir.AluOpType.add, maximum
                         )

@@ -29,34 +29,36 @@ def tile_lookup_maxgate_relu_kernel(tc, tab, y, w, b, offs, out):
         offsets = held.tile([P, picks // 16], U16)
         nc.sync.dma_start(offsets[:], offs)
 
-        weights = [held.tile([P, outs], BF16, name=f"weights{k}") for k in range(row_blocks)]
+        weights = held.tile([P, row_blocks, outs], BF16)
         bias = held.tile([P, out_blocks], F32)
         floors, gates, stream = [], [], []
         for k in range(row_blocks):
             block = slice(k * P, (k + 1) * P)
             floors.append(held.tile([P, places], F32, name=f"floors{k}"))
             gates.append(held.tile([P, places], F32, name=f"gates{k}"))
-            stream.append([held.tile([P, PIECE], F32, name=f"stream{k}_{c}") for c in range(pieces)])
-            pieces_ahead = pieces if k < row_blocks - 1 else 1
+            stream.append(held.tile([P, picks], F32, name=f"stream{k}"))
             nc.sync.dma_start(floors[k][:], tab[0, block, :])
-            for c in range(pieces_ahead):
-                nc.sync.dma_start(stream[k][c][:], y[block, c * PIECE : (c + 1) * PIECE])
-            nc.sync.dma_start(gates[k][:], tab[1, block, :])
-            for c in range(pieces_ahead, pieces):
-                nc.sync.dma_start(stream[k][c][:], y[block, c * PIECE : (c + 1) * PIECE])
-            if k == 0:
-                for i in range(row_blocks):
-                    nc.sync.dma_start(weights[i][:], w[i * P : (i + 1) * P, :])
-        nc.scalar.dma_start(bias[:], b.rearrange("(m p) one -> p (m one)", p=P))
+            if k < row_blocks - 1:
+                nc.sync.dma_start(stream[k][:], y[block, :])
+                nc.sync.dma_start(gates[k][:], tab[1, block, :])
+            else:
+                nc.sync.dma_start(weights[:], w.rearrange("(k p) m -> p k m", p=P))
+                for c in range(pieces):
+                    if c == 1:
+                        nc.sync.dma_start(gates[k][:], tab[1, block, :])
+                    cols = slice(c * PIECE, (c + 1) * PIECE)
+                    nc.sync.dma_start(stream[k][:, cols], y[block, cols])
+        nc.scalar.dma_start(bias[:], b.rearrange("(p m) one -> p (m one)", p=P))
 
         sums = [[psum.tile([P, PIECE], F32, name=f"sum{m}_{c}") for c in range(pieces)] for m in range(out_blocks)]
 
         for k in range(row_blocks):
             for c in range(pieces):
+                cols = slice(c * PIECE, (c + 1) * PIECE)
                 picked = offsets[:, c * PIECE // 16 : (c + 1) * PIECE // 16]
 
                 floored = work.tile([P, PIECE], F32)
-                nc.vector.tensor_tensor(floored[:], floors[k][:].indirect(picked), stream[k][c][:], maximum)
+                nc.vector.tensor_tensor(floored[:], floors[k][:].indirect(picked), stream[k][:, cols], maximum)
                 gate = work.tile([P, PIECE], F32)
                 nc.scalar.activation(gate[:], gates[k][:].indirect(picked), tanh)
                 x = work.tile([P, PIECE], BF16)
@@ -65,7 +67,7 @@ def tile_lookup_maxgate_relu_kernel(tc, tab, y, w, b, offs, out):
                 for m in range(out_blocks):
                     nc.tensor.matmul(
                         sums[m][c][:],
-                        weights[k][:, m * P : (m + 1) * P],
+                        weights[:, k, m:outs:out_blocks],
                         x[:],
                         start=(k == 0),
                         stop=(k == row_blocks - 1),
@@ -73,7 +75,6 @@ def tile_lookup_maxgate_relu_kernel(tc, tab, y, w, b, offs, out):
                 if k < row_blocks - 1:
                     continue
 
-                cols = slice(c * PIECE, (c + 1) * PIECE)
                 for m in range(out_blocks):
                     result = work.tile([P, PIECE], F32, name=f"result{m}")
                     if c == pieces - 1 and m % 2 == 0:
@@ -82,4 +83,4 @@ def tile_lookup_maxgate_relu_kernel(tc, tab, y, w, b, offs, out):
                         )
                     else:
                         nc.scalar.activation(result[:], sums[m][c][:], relu, bias=bias[:, m : m + 1])
-                    nc.sync.dma_start(out[m * P : (m + 1) * P, cols], result[:])
+                    nc.sync.dma_start(out.rearrange("(p m) j -> m p j", p=P)[m, :, cols], result[:])

import concourse.mybir as mybir

P = 128
PIECE = 512
FLOPS = 2 * 256 * 256 * 1536
F32, BF16, U16 = mybir.dt.float32, mybir.dt.bfloat16, mybir.dt.uint16


def tile_lookup_maxgate_relu_kernel(tc, tab, y, w, b, offs, out):
    nc = tc.nc
    maximum, mult = mybir.AluOpType.max, mybir.AluOpType.mult
    tanh, relu = mybir.ActivationFunctionType.Tanh, mybir.ActivationFunctionType.Relu

    rows, places = tab.shape[1], tab.shape[2]
    picks = y.shape[1]
    outs = w.shape[1]
    row_blocks, out_blocks, pieces = rows // P, outs // P, picks // PIECE

    with (
        tc.tile_pool(name="held", bufs=1) as held,
        tc.tile_pool(name="work", bufs=pieces) as work,
        tc.psum_pool(name="psum", bufs=1) as psum,
    ):
        zeros = held.tile([P, 1], F32)
        nc.vector.memset(zeros[:], 0.0)
        warm_up = held.tile([P, 1], F32)
        nc.scalar.activation(warm_up[:], zeros[:], tanh)

        offsets = held.tile([P, picks // 16], U16)
        nc.sync.dma_start(offsets[:], offs)

        weights = held.tile([P, row_blocks, outs], BF16)
        bias = held.tile([P, out_blocks], F32)
        floors, gates, stream = [], [], []
        for k in range(row_blocks):
            block = slice(k * P, (k + 1) * P)
            floors.append(held.tile([P, places], F32, name=f"floors{k}"))
            gates.append(held.tile([P, places], F32, name=f"gates{k}"))
            stream.append(held.tile([P, picks], F32, name=f"stream{k}"))
            nc.sync.dma_start(floors[k][:], tab[0, block, :])
            if k < row_blocks - 1:
                nc.sync.dma_start(stream[k][:], y[block, :])
                nc.sync.dma_start(gates[k][:], tab[1, block, :])
            else:
                nc.sync.dma_start(weights[:], w.rearrange("(k p) m -> p k m", p=P))
                for c in range(pieces):
                    if c == 1:
                        nc.sync.dma_start(gates[k][:], tab[1, block, :])
                    cols = slice(c * PIECE, (c + 1) * PIECE)
                    nc.sync.dma_start(stream[k][:, cols], y[block, cols])
        nc.scalar.dma_start(bias[:], b.rearrange("(p m) one -> p (m one)", p=P))

        sums = [[psum.tile([P, PIECE], F32, name=f"sum{m}_{c}") for c in range(pieces)] for m in range(out_blocks)]

        for k in range(row_blocks):
            for c in range(pieces):
                cols = slice(c * PIECE, (c + 1) * PIECE)
                picked = offsets[:, c * PIECE // 16 : (c + 1) * PIECE // 16]

                floored = work.tile([P, PIECE], F32)
                nc.vector.tensor_tensor(floored[:], floors[k][:].indirect(picked), stream[k][:, cols], maximum)
                gate = work.tile([P, PIECE], F32)
                nc.scalar.activation(gate[:], gates[k][:].indirect(picked), tanh)
                x = work.tile([P, PIECE], BF16)
                nc.vector.tensor_tensor(x[:], floored[:], gate[:], mult)

                for m in range(out_blocks):
                    nc.tensor.matmul(
                        sums[m][c][:],
                        weights[:, k, m:outs:out_blocks],
                        x[:],
                        start=(k == 0),
                        stop=(k == row_blocks - 1),
                    )
                if k < row_blocks - 1:
                    continue

                for m in range(out_blocks):
                    result = work.tile([P, PIECE], F32, name=f"result{m}")
                    if c == pieces - 1 and m % 2 == 0:
                        nc.vector.tensor_scalar(
                            result[:], sums[m][c][:], bias[:, m : m + 1], 0.0, mybir.AluOpType.add, maximum
                        )
                    else:
                        nc.scalar.activation(result[:], sums[m][c][:], relu, bias=bias[:, m : m + 1])
                    nc.sync.dma_start(out.rearrange("(p m) j -> m p j", p=P)[m, :, cols], result[:])
